import numpy as np
import ml_dtypes


def mxq(x, axis, fmt="e4m3"):
    dtype, down = {"e4m3": (ml_dtypes.float8_e4m3fn, 7), "e5m2": (ml_dtypes.float8_e5m2, 14)}[fmt]
    v = np.moveaxis(np.asarray(x, np.float32).astype(ml_dtypes.bfloat16).astype(np.float64), axis, -1)
    blocks = v.reshape(v.shape[:-1] + (-1, 32))
    amax = np.abs(blocks).max(-1, keepdims=True)
    byte = np.maximum(np.where(amax > 0, np.frexp(amax)[1] - 1 + 127, 0) - down, 1)
    scale = np.exp2(byte - 127.0)
    codes = (blocks / scale).astype(np.float32).astype(dtype).astype(np.float64)
    return np.moveaxis((codes * scale).reshape(v.shape), -1, axis)


WIDE = False


def mx_kscale(k):
    if not WIDE:
        return np.ones(k)
    levels = np.array([10, -10, 5, -5, 0])
    if k % 512:
        return np.exp2(np.random.permutation(np.resize(levels, k // 32))).repeat(32)
    a = np.empty((k // 512, 16))
    for p in range(k // 512):
        a[p, :8] = np.random.permutation(np.resize(levels, 8))
        for g in range(8):
            far = levels[np.abs(levels - a[p, g]) >= 10]
            a[p, g + 8] = far[np.random.randint(len(far))]
    return np.exp2(a.ravel()).repeat(32)


def f64(x):
    return np.asarray(x).astype(np.float64)


def striped(idx):
    return np.tile(idx.reshape(-1, 16).T, (8, 1)).astype(np.uint16)


def unstriped(offs):
    return offs[:16].T.reshape(-1).astype(np.int64)


E2M1 = np.array([0.0, 0.5, 1.0, 1.5, 2.0, 3.0, 4.0, 6.0, -0.0, -0.5, -1.0, -1.5, -2.0, -3.0, -4.0, -6.0])


def pack_weight(w, fmt):
    k, n = w.shape
    w = f64(np.asarray(w, np.float32).astype(ml_dtypes.bfloat16)).reshape(k // 32, 32, n)
    amax = np.abs(w).max(1)
    if fmt == "e4m3":
        byte = np.frexp(amax)[1] - 1 + 127 - 7
    else:
        mant, ex = np.frexp(amax / 6.0)
        byte = np.where(mant > 0.5, ex, ex - 1) + 127
    byte = np.clip(np.where(amax > 0, byte, 1), 1, 254)
    scaled = (w * np.exp2(127.0 - byte)[:, None, :]).reshape(k, n).astype(np.float32)
    by_word = np.ascontiguousarray(scaled.reshape(k // 512, 128, 4, n).transpose(0, 1, 3, 2))
    if fmt == "e4m3":
        words = by_word.astype(ml_dtypes.float8_e4m3fn).view(np.uint8)
    else:
        c = by_word.astype(ml_dtypes.float4_e2m1fn).view(np.uint8) & 0xF
        words = (c[..., 0::2] | (c[..., 1::2] << 4)).reshape(k // 512, 128, 2 * n)
    return np.ascontiguousarray(words), np.ascontiguousarray(byte.astype(np.uint8).reshape(k // 512, 16, n))


def unpack_weight(words, scales, fmt):
    g, _, n = scales.shape
    words = np.ascontiguousarray(words).reshape(g, 128, n, -1)
    if fmt == "e4m3":
        vals = words.view(ml_dtypes.float8_e4m3fn).astype(np.float64)
    else:
        nib = np.empty((g, 128, n, 4), np.uint8)
        nib[..., 0::2] = words & 0xF
        nib[..., 1::2] = words >> 4
        vals = E2M1[nib]
    vals = vals * np.repeat(np.exp2(scales.astype(np.float64) - 127.0), 8, axis=1)[..., None]
    return vals.transpose(0, 1, 3, 2).reshape(g * 512, n)


K, T, S1, S2 = 512, 2048, 1024, 1024


def setup_inputs():
    n = np.random.standard_normal
    s = mx_kscale(K)
    u = mx_kscale(K)
    first, second = np.random.permutation(T)[:S1], np.random.permutation(T)[:S2]
    xf = n((K, T))
    x = pack_weight(xf * s[:, None], "e4m3")
    w1 = pack_weight(n((K, K)) / np.sqrt(K) / s[:, None] * u, "e2m1")
    w2 = pack_weight(n((K, K)) / np.sqrt(K) / u[:, None] * u, "e4m3")
    return {
        "x_words": x[0],
        "x_scales": x[1],
        "xr": (xf * u[:, None]).astype(np.float32),
        "w1_words": w1[0],
        "w1_scales": w1[1],
        "w2_words": w2[0],
        "w2_scales": w2[1],
        "gate1": (np.tile(np.random.uniform(0.2, 1.0, S1), (128, 1))).astype(np.float32),
        "gate2": (np.tile(np.random.uniform(0.2, 1.0, S2), (128, 1))).astype(np.float32),
        "offs": striped(first),
        "offs2": striped(second),
    }


def reference(x_words, x_scales, xr, w1_words, w1_scales, w2_words, w2_scales, gate1, gate2, offs, offs2):
    w1 = unpack_weight(w1_words, w1_scales, "e2m1")
    w2 = unpack_weight(w2_words, w2_scales, "e4m3")
    idx, idx2 = unstriped(offs), unstriped(offs2)
    r = f64(xr)
    r[:, idx] += f64(gate1[:1]) * (w1.T @ unpack_weight(x_words, x_scales, "e4m3")[:, idx])
    r2 = r.copy()
    r2[:, idx2] += f64(gate2[:1]) * (w2.T @ mxq(r[:, idx2], 0, "e4m3"))
    return r2

@@ -1,0 +1,205 @@
+from contextlib import ExitStack
+
+import concourse.mybir as mybir
+
+K, T, S = 512, 2048, 1024
+FLOPS = 2 * 2 * K * K * S
+
+F32 = mybir.dt.float32
+BF16 = mybir.dt.bfloat16
+I32 = mybir.dt.int32
+U32 = mybir.dt.uint32
+U16 = mybir.dt.uint16
+U8 = mybir.dt.uint8
+FP8X4 = mybir.dt.float8_e4m3fn_x4
+FP4X4 = mybir.dt.float4_e2m1fn_x4
+MULT = mybir.AluOpType.mult
+ADD = mybir.AluOpType.add
+COPY = mybir.ActivationFunctionType.Copy
+
+P = 128
+PLANES = 4
+PER_COL = 16
+QUARTER = S // 4
+BANK = 512
+CHUNK = 512
+
+
+def span(i, width):
+    return slice(i * width, (i + 1) * width)
+
+
+def tile_moe_mod_none_kernel(
+    tc, x_words, x_scales, xr, w1_words, w1_scales, w2_words, w2_scales, gate1, gate2, offs, offs2, out
+):
+    nc = tc.nc
+    xr_planes = xr.rearrange("(p t) n -> p t n", t=PLANES)
+    out_planes = out.rearrange("(p t) n -> p t n", t=PLANES)
+
+    with ExitStack() as ctx:
+        keep = ctx.enter_context(tc.tile_pool(name="keep", bufs=1))
+        windows = ctx.enter_context(tc.tile_pool(name="windows", bufs=PLANES))
+        psum = ctx.enter_context(tc.psum_pool(name="psum", bufs=8))
+
+        list1 = keep.tile([P, S // PER_COL], U16, name="list1")
+        list2 = keep.tile([P, S // PER_COL], U16, name="list2")
+        xw = keep.tile([P, T], I32, name="xw", tag="a", align_bytes=64)
+        xs = keep.tile([P, T], U8, name="xs", tag="b", align_bytes=64)
+        xw_slots = keep.tile([P, S], U32, name="xw_slots", tag="c", align_bytes=64)
+        xs_slots = keep.tile([P, S], U8, name="xs_slots", tag="d", align_bytes=64)
+        w1_raw = keep.tile([P, 2 * K], U8, name="w1_raw", tag="e", align_bytes=64)
+        ws_raw = keep.tile([P, K], U8, name="ws_raw")
+        w1 = keep.tile([P, 2 * K], U8, name="w1", tag="f", align_bytes=64)
+        w1s = keep.tile([P, K], U8, name="w1s", align_bytes=64)
+        w2 = keep.tile([P, K], I32, name="w2", align_bytes=64)
+        w2s = keep.tile([P, K], U8, name="w2s", align_bytes=64)
+        g1 = keep.tile([P, S], F32, name="g1")
+        zero = keep.tile([P, 8], F32, name="zero")
+        res_bf = [keep.tile([P, T], BF16, name="res_bf%d" % t) for t in range(PLANES)]
+        sums = [keep.tile([P, S], F32, name="sums%d" % t) for t in range(PLANES)]
+        gated = [keep.tile([P, S], F32, name="gated%d" % t) for t in range(PLANES)]
+        picked = keep.tile([P, S, PLANES], BF16, name="picked", align_bytes=64)
+        rw = keep.tile([P, S], U32, name="rw", align_bytes=64)
+        rs = keep.tile([P, S], U8, name="rs", align_bytes=64)
+
+        def load_scales(plane, rows):
+            for q in range(4):
+                nc.sync.dma_start(plane[32 * q : 32 * q + 4, :].bitcast(I32), rows[0, span(q, 4), :].bitcast(I32))
+
+        def offsets(lst, slots):
+            return lst[:, slots.start // PER_COL : slots.stop // PER_COL]
+
+        def by_plane(dst, src):
+            nc.vector.tensor_copy(
+                dst.rearrange("p (t m) -> p t m", t=PLANES), src.rearrange("p (m t) -> p t m", t=PLANES)
+            )
+
+        def scalar_zero(window):
+            for c in range(T // CHUNK):
+                nc.scalar.activation(window[:, span(c, CHUNK)], zero[:, 0:1].to_broadcast([P, CHUNK]), COPY)
+
+        nc.vector.memset(xs[:].bitcast(I32), 0)
+        nc.vector.memset(zero[:], 0.0)
+        nc.vector.memset(ws_raw[:].bitcast(I32), 0)
+        nc.sync.dma_start(list1[:], offs)
+        nc.sync.dma_start(xw[:], x_words[0].rearrange("p t d -> p (t d)").bitcast(I32))
+        nc.sync.dma_start(w1_raw[:].bitcast(I32), w1_words[0].bitcast(I32))
+        load_scales(xs, x_scales)
+        load_scales(ws_raw, w1_scales)
+        nc.sync.dma_start(g1[:], gate1)
+        nc.sync.dma_start(list2[:], offs2)
+
+        win1 = [windows.tile([P, T], F32, name="win", tag="win") for t in range(PLANES)]
+        scalar_zero(win1[0])
+        scalar_zero(win1[1])
+        nc.vector.memset(win1[2][:], 0.0)
+        nc.vector.memset(win1[3][:], 0.0)
+
+        nc.vector.tensor_copy(xw_slots[:], xw[:].bitcast(U32).indirect(list1[:]))
+        by_plane(w1[:].bitcast(U16), w1_raw[:].bitcast(U16))
+        by_plane(w1s[:], ws_raw[:])
+
+        def product(words, scales, w_words, w_scales, t, slots):
+            bank = psum.tile([P, slots.stop - slots.start], F32, name="bank", tag="bank")
+            nc.tensor.matmul_mx(
+                bank[:],
+                lhsT=w_words,
+                lhsT_scale=w_scales[:, span(t, P)],
+                rhs=words[:, slots].bitcast(FP8X4),
+                rhs_scale=scales[:, slots],
+                start=True,
+                stop=True,
+            )
+            return bank
+
+        def product1(t, slots):
+            return product(xw_slots, xs_slots, w1[:, span(t, 2 * P)].bitcast(FP4X4), w1s, t, slots)
+
+        def product2(t, slots):
+            return product(rw, rs, w2[:, span(t, P)].bitcast(FP8X4), w2s, t, slots)
+
+        for q in range(4):
+            slots = span(q, QUARTER)
+            nc.vector.tensor_copy(xs_slots[:, slots], xs[:].indirect(offsets(list1, slots)))
+        res = []
+
+        def load_plane(tag):
+            res.append(keep.tile([P, T], F32, name="res", tag=tag, align_bytes=64))
+            nc.sync.dma_start(res[-1][:], xr_planes[:, len(res) - 1, :])
+
+        load_plane("e")
+        load_plane("a")
+        load_plane("b")
+        for q in range(4):
+            slots = span(q, QUARTER)
+            nc.scalar.copy(sums[0][:, slots], product1(0, slots)[:])
+            nc.gpsimd.tensor_tensor(gated[0][:, slots], sums[0][:, slots], g1[:, slots], MULT)
+            nc.vector.tensor_copy(win1[0][:].indirect(offsets(list1, slots)), gated[0][:, slots])
+
+        def gate_plane(prod, gate, t):
+            for h in range(S // BANK):
+                slots = span(h, BANK)
+                nc.scalar.copy(sums[t][:, slots], prod(t, slots)[:])
+                nc.gpsimd.tensor_tensor(gated[t][:, slots], sums[t][:, slots], gate[:, slots], MULT)
+
+        gate_plane(product1, g1, 1)
+        for t in range(1, PLANES):
+            if t + 1 < PLANES:
+                gate_plane(product1, g1, t + 1)
+            if t + 1 == PLANES - 1:
+                load_plane("d")
+                w2_raw = keep.tile([P, K], I32, name="w2_raw", tag="f", align_bytes=64)
+                g2 = keep.tile([P, S], F32, name="g2", tag="c", align_bytes=64)
+                nc.sync.dma_start(w2_raw[:], w2_words[0].rearrange("p n d -> p (n d)").bitcast(I32))
+                load_scales(ws_raw, w2_scales)
+                nc.sync.dma_start(g2[:], gate2)
+            nc.vector.tensor_copy(win1[t][:].indirect(list1[:]), gated[t][:])
+            done = t - 1
+            for c in range(T // CHUNK):
+                cols = span(c, CHUNK)
+                nc.gpsimd.tensor_tensor(res[done][:, cols], res[done][:, cols], win1[done][:, cols], ADD)
+                nc.scalar.copy(res_bf[done][:, cols], res[done][:, cols])
+            nc.scalar.activation(picked[:, :, done], res_bf[done][:].indirect(list2[:]), COPY)
+
+        last = PLANES - 1
+        nc.vector.tensor_tensor(res_bf[last][:], res[last][:], win1[last][:], ADD)
+        by_plane(w2[:], w2_raw[:])
+        by_plane(w2s[:], ws_raw[:])
+
+        win2 = [windows.tile([P, T], F32, name="win", tag="win") for t in range(last)]
+        scalar_zero(win2[0])
+        for q in range(4):
+            slots = span(q, QUARTER)
+            nc.scalar.activation(picked[:, slots, last], res_bf[last][:].indirect(offsets(list2, slots)), COPY)
+            nc.vector.quantize_mx(
+                rw[:, slots].bitcast(FP8X4), rs[:, slots], picked[:, slots, :].rearrange("p s t -> p (s t)")
+            )
+            nc.vector.tensor_tensor(gated[0][:, slots], product2(0, slots)[:], g2[:, slots], MULT)
+            nc.vector.tensor_copy(win2[0][:].indirect(offsets(list2, slots)), gated[0][:, slots])
+        for c in range(T // CHUNK):
+            cols = span(c, CHUNK)
+            nc.vector.tensor_tensor(res[last][:, cols], res[last][:, cols], win1[last][:, cols], ADD)
+        win2.append(windows.tile([P, T], F32, name="win", tag="win"))
+
+        def gate_whole(t):
+            for h in range(S // BANK):
+                slots = span(h, BANK)
+                nc.scalar.copy(sums[t][:, slots], product2(t, slots)[:])
+            nc.gpsimd.tensor_tensor(gated[t][:], sums[t][:], g2[:], MULT)
+
+        gate_whole(1)
+        scalar_zero(win2[1])
+        for t in range(1, PLANES):
+            if t + 1 < PLANES:
+                gate_whole(t + 1)
+                scalar_zero(win2[t + 1])
+            nc.vector.tensor_copy(win2[t][:].indirect(list2[:]), gated[t][:])
+            done = t - 1
+            for c in range(T // CHUNK):
+                cols = span(c, CHUNK)
+                nc.gpsimd.tensor_tensor(res[done][:, cols], res[done][:, cols], win2[done][:, cols], ADD)
+            nc.sync.dma_start(out_planes[:, done, :], res[done][:])
+        for c in range(T // CHUNK):
+            cols = span(c, CHUNK)
+            nc.vector.tensor_tensor(res[last][:, cols], res[last][:, cols], win2[last][:, cols], ADD)
+            nc.sync.dma_start(out_planes[:, last, cols], res[last][:, cols])

@@ -19,14 +19,23 @@ COPY = mybir.ActivationFunctionType.Copy
 
 P = 128
 PLANES = 4
+LAST = PLANES - 1
 PER_COL = 16
-QUARTER = S // 4
 BANK = 512
-CHUNK = 512
 
 
 def span(i, width):
     return slice(i * width, (i + 1) * width)
+
+
+def cuts(total, width):
+    return [span(i, width) for i in range(total // width)]
+
+
+PIECES1 = [slice(0, 256), slice(256, 512), slice(512, 1024)]
+QUARTERS = cuts(S, 256)
+HALVES = cuts(S, BANK)
+TAIL = [slice(0, 640), slice(640, 1280), slice(1280, 1792), slice(1792, 2048)]
 
 
 def tile_moe_mod_none_kernel(
@@ -38,33 +47,35 @@ def tile_moe_mod_none_kernel(
 
     with ExitStack() as ctx:
         keep = ctx.enter_context(tc.tile_pool(name="keep", bufs=1))
-        windows = ctx.enter_context(tc.tile_pool(name="windows", bufs=PLANES))
         psum = ctx.enter_context(tc.psum_pool(name="psum", bufs=8))
+
+        def shared(shape, dtype, name, tag):
+            return keep.tile(shape, dtype, name=name, tag=tag, align_bytes=64)
 
         list1 = keep.tile([P, S // PER_COL], U16, name="list1")
         list2 = keep.tile([P, S // PER_COL], U16, name="list2")
-        xw = keep.tile([P, T], I32, name="xw", tag="a", align_bytes=64)
-        xs = keep.tile([P, T], U8, name="xs", tag="b", align_bytes=64)
-        xw_slots = keep.tile([P, S], U32, name="xw_slots", tag="c", align_bytes=64)
-        xs_slots = keep.tile([P, S], U8, name="xs_slots", tag="d", align_bytes=64)
-        w1_raw = keep.tile([P, 2 * K], U8, name="w1_raw", tag="e", align_bytes=64)
-        ws_raw = keep.tile([P, K], U8, name="ws_raw")
-        w1 = keep.tile([P, 2 * K], U8, name="w1", tag="f", align_bytes=64)
-        w1s = keep.tile([P, K], U8, name="w1s", align_bytes=64)
-        w2 = keep.tile([P, K], I32, name="w2", align_bytes=64)
-        w2s = keep.tile([P, K], U8, name="w2s", align_bytes=64)
+        xw = shared([P, T], I32, "xw", "a")
+        xs = shared([P, T], U8, "xs", "b")
+        xs_slots = shared([P, S], U8, "xs_slots", "c")
+        w1_raw = shared([P, 2 * K], U8, "w1_raw", "d")
+        w1s_raw = shared([P, K], U8, "w1s_raw", "e")
+        w1 = shared([P, 2 * K], U8, "w1", "f")
+        w1s = shared([P, K], U8, "w1s", "g")
         g1 = keep.tile([P, S], F32, name="g1")
         zero = keep.tile([P, 8], F32, name="zero")
-        res_bf = [keep.tile([P, T], BF16, name="res_bf%d" % t) for t in range(PLANES)]
-        sums = [keep.tile([P, S], F32, name="sums%d" % t) for t in range(PLANES)]
+        res_bf = [keep.tile([P, T], BF16, name="res_bf%d" % t) for t in range(LAST)]
+        sums = [shared([P, S], F32, "sums", "sums%d" % t) for t in range(PLANES)]
         gated = [keep.tile([P, S], F32, name="gated%d" % t) for t in range(PLANES)]
-        picked = keep.tile([P, S, PLANES], BF16, name="picked", align_bytes=64)
+        picked = shared([P, S, PLANES], BF16, "picked", "picked")
         rw = keep.tile([P, S], U32, name="rw", align_bytes=64)
         rs = keep.tile([P, S], U8, name="rs", align_bytes=64)
 
         def load_scales(plane, rows):
             for q in range(4):
-                nc.sync.dma_start(plane[32 * q : 32 * q + 4, :].bitcast(I32), rows[0, span(q, 4), :].bitcast(I32))
+                four = rows[0, span(q, 4), :].bitcast(I32)
+                nc.sync.dma_start(
+                    plane[span(q, 32), :].bitcast(I32), four.unsqueeze(0).broadcast_to([8, 4, four.shape[1]])
+                )
 
         def offsets(lst, slots):
             return lst[:, slots.start // PER_COL : slots.stop // PER_COL]
@@ -75,131 +86,185 @@ def tile_moe_mod_none_kernel(
             )
 
         def scalar_zero(window):
-            for c in range(T // CHUNK):
-                nc.scalar.activation(window[:, span(c, CHUNK)], zero[:, 0:1].to_broadcast([P, CHUNK]), COPY)
+            for cols in cuts(T, 512):
+                nc.scalar.activation(window[:, cols], zero[:, 0:1].to_broadcast([P, 512]), COPY)
 
-        nc.vector.memset(xs[:].bitcast(I32), 0)
+        def product(bank, w_words, w_scales, words, scales):
+            nc.tensor.matmul_mx(
+                bank, lhsT=w_words, lhsT_scale=w_scales, rhs=words.bitcast(FP8X4), rhs_scale=scales, start=True, stop=True
+            )
+
+        def new_bank(width):
+            return psum.tile([P, width], F32, name="bank", tag="bank")
+
+        def new_plane(name, tag):
+            return shared([P, T], F32, name, tag)
+
+        def gate_on_gpsimd(t, gate, slots):
+            nc.gpsimd.tensor_tensor(gated[t][:, slots], sums[t][:, slots], gate[:, slots], MULT)
+
+        def scatter(window, lst, t, slots):
+            nc.vector.tensor_copy(window[:].indirect(offsets(lst, slots)), gated[t][:, slots])
+
         nc.vector.memset(zero[:], 0.0)
-        nc.vector.memset(ws_raw[:].bitcast(I32), 0)
-        nc.sync.dma_start(list1[:], offs)
-        nc.sync.dma_start(xw[:], x_words[0].rearrange("p t d -> p (t d)").bitcast(I32))
         nc.sync.dma_start(w1_raw[:].bitcast(I32), w1_words[0].bitcast(I32))
         load_scales(xs, x_scales)
-        load_scales(ws_raw, w1_scales)
+        nc.sync.dma_start(list1[:], offs)
+        nc.sync.dma_start(xw[:], x_words[0].rearrange("p t d -> p (t d)").bitcast(I32))
+        load_scales(w1s_raw, w1_scales)
         nc.sync.dma_start(g1[:], gate1)
         nc.sync.dma_start(list2[:], offs2)
 
-        win1 = [windows.tile([P, T], F32, name="win", tag="win") for t in range(PLANES)]
+        win1 = [new_plane("win1", "win%d" % t) for t in range(PLANES)]
+        win2 = [new_plane("win2", "win4")]
         scalar_zero(win1[0])
         scalar_zero(win1[1])
-        nc.vector.memset(win1[2][:], 0.0)
         nc.vector.memset(win1[3][:], 0.0)
+        nc.vector.memset(win1[2][:], 0.0)
+        for half in cuts(T, 1024):
+            nc.gpsimd.tensor_scalar(win2[0][:, half], win1[2][:, half], 1.0, 0.0, MULT, ADD)
 
-        nc.vector.tensor_copy(xw_slots[:], xw[:].bitcast(U32).indirect(list1[:]))
         by_plane(w1[:].bitcast(U16), w1_raw[:].bitcast(U16))
-        by_plane(w1s[:], ws_raw[:])
+        nc.vector.tensor_copy(xs_slots[:], xs[:].indirect(list1[:]))
+        by_plane(w1s[:], w1s_raw[:])
+        xw_slots = []
+        for slots, tag in zip(PIECES1, "hde"):
+            xw_slots.append(shared([P, slots.stop - slots.start], U32, "xw_slots", tag))
+            nc.vector.tensor_copy(xw_slots[-1][:], xw[:].bitcast(U32).indirect(offsets(list1, slots)))
 
-        def product(words, scales, w_words, w_scales, t, slots):
-            bank = psum.tile([P, slots.stop - slots.start], F32, name="bank", tag="bank")
-            nc.tensor.matmul_mx(
-                bank[:],
-                lhsT=w_words,
-                lhsT_scale=w_scales[:, span(t, P)],
-                rhs=words[:, slots].bitcast(FP8X4),
-                rhs_scale=scales[:, slots],
-                start=True,
-                stop=True,
-            )
-            return bank
-
-        def product1(t, slots):
-            return product(xw_slots, xs_slots, w1[:, span(t, 2 * P)].bitcast(FP4X4), w1s, t, slots)
-
-        def product2(t, slots):
-            return product(rw, rs, w2[:, span(t, P)].bitcast(FP8X4), w2s, t, slots)
-
-        for q in range(4):
-            slots = span(q, QUARTER)
-            nc.vector.tensor_copy(xs_slots[:, slots], xs[:].indirect(offsets(list1, slots)))
         res = []
 
         def load_plane(tag):
-            res.append(keep.tile([P, T], F32, name="res", tag=tag, align_bytes=64))
+            res.append(shared([P, T], F32, "res", tag))
             nc.sync.dma_start(res[-1][:], xr_planes[:, len(res) - 1, :])
 
-        load_plane("e")
-        load_plane("a")
         load_plane("b")
-        for q in range(4):
-            slots = span(q, QUARTER)
-            nc.scalar.copy(sums[0][:, slots], product1(0, slots)[:])
-            nc.gpsimd.tensor_tensor(gated[0][:, slots], sums[0][:, slots], g1[:, slots], MULT)
-            nc.vector.tensor_copy(win1[0][:].indirect(offsets(list1, slots)), gated[0][:, slots])
+        load_plane("a")
 
-        def gate_plane(prod, gate, t):
-            for h in range(S // BANK):
-                slots = span(h, BANK)
-                nc.scalar.copy(sums[t][:, slots], prod(t, slots)[:])
-                nc.gpsimd.tensor_tensor(gated[t][:, slots], sums[t][:, slots], gate[:, slots], MULT)
+        def product1(bank, t, piece):
+            product(
+                bank,
+                w1[:, span(t, 2 * P)].bitcast(FP4X4),
+                w1s[:, span(t, P)],
+                xw_slots[piece][:],
+                xs_slots[:, PIECES1[piece]],
+            )
 
-        gate_plane(product1, g1, 1)
-        for t in range(1, PLANES):
-            if t + 1 < PLANES:
-                gate_plane(product1, g1, t + 1)
-            if t + 1 == PLANES - 1:
-                load_plane("d")
-                w2_raw = keep.tile([P, K], I32, name="w2_raw", tag="f", align_bytes=64)
-                g2 = keep.tile([P, S], F32, name="g2", tag="c", align_bytes=64)
-                nc.sync.dma_start(w2_raw[:], w2_words[0].rearrange("p n d -> p (n d)").bitcast(I32))
-                load_scales(ws_raw, w2_scales)
-                nc.sync.dma_start(g2[:], gate2)
-            nc.vector.tensor_copy(win1[t][:].indirect(list1[:]), gated[t][:])
-            done = t - 1
-            for c in range(T // CHUNK):
-                cols = span(c, CHUNK)
-                nc.gpsimd.tensor_tensor(res[done][:, cols], res[done][:, cols], win1[done][:, cols], ADD)
-                nc.scalar.copy(res_bf[done][:, cols], res[done][:, cols])
-            nc.scalar.activation(picked[:, :, done], res_bf[done][:].indirect(list2[:]), COPY)
+        for piece, slots in enumerate(PIECES1):
+            bank = new_bank(slots.stop - slots.start)
+            product1(bank[:], 0, piece)
+            if piece == 0:
+                nc.vector.tensor_tensor(gated[0][:, slots], bank[:], g1[:, slots], MULT)
+            else:
+                nc.scalar.copy(sums[0][:, slots], bank[:])
+                gate_on_gpsimd(0, g1, slots)
+            scatter(win1[0], list1, 0, slots)
 
-        last = PLANES - 1
-        nc.vector.tensor_tensor(res_bf[last][:], res[last][:], win1[last][:], ADD)
-        by_plane(w2[:], w2_raw[:])
-        by_plane(w2s[:], ws_raw[:])
+        def gate_plane1(t):
+            low, high = new_bank(BANK), new_bank(BANK)
+            product1(low[:, PIECES1[0]], t, 0)
+            product1(low[:, PIECES1[1]], t, 1)
+            product1(high[:], t, 2)
+            nc.scalar.copy(sums[t][:, HALVES[0]], low[:])
+            nc.scalar.copy(sums[t][:, HALVES[1]], high[:])
+            gate_on_gpsimd(t, g1, slice(0, S))
 
-        win2 = [windows.tile([P, T], F32, name="win", tag="win") for t in range(last)]
-        scalar_zero(win2[0])
-        for q in range(4):
-            slots = span(q, QUARTER)
-            nc.scalar.activation(picked[:, slots, last], res_bf[last][:].indirect(offsets(list2, slots)), COPY)
+        def finish_plane1(t, total):
+            for half in cuts(T, 1024):
+                nc.gpsimd.tensor_tensor(total[:, half], res[t][:, half], win1[t][:, half], ADD)
+            for cols in cuts(T, 512):
+                nc.scalar.copy(res_bf[t][:, cols], total[:, cols])
+            res[t] = total
+
+        def pick(t, slots):
+            nc.scalar.activation(picked[:, slots, t], res_bf[t][:].indirect(offsets(list2, slots)), COPY)
+
+        gate_plane1(1)
+        gate_plane1(2)
+        scatter(win1[1], list1, 1, slice(0, S))
+        finish_plane1(0, new_plane("res", "sums2"))
+        gate_plane1(3)
+        load_plane("c")
+        w2_raw = shared([P, K], I32, "w2_raw", "f")
+        w2s_raw = shared([P, K], U8, "w2s_raw", "g")
+        g2 = shared([P, S], F32, "g2", "h")
+        xr_last = [shared([P, 1024], F32, "xr_last", tag) for tag in "de"]
+        for tile, half in zip(xr_last, cuts(T, 1024)):
+            nc.sync.dma_start(tile[:], xr_planes[:, LAST, half])
+        nc.sync.dma_start(w2_raw[:], w2_words[0].rearrange("p n d -> p (n d)").bitcast(I32))
+        load_scales(w2s_raw, w2_scales)
+        nc.sync.dma_start(g2[:], gate2)
+        load_plane("b")
+        pick(0, slice(0, S))
+        scatter(win1[2], list1, 2, slice(0, S))
+        finish_plane1(1, new_plane("res", "sums3"))
+        pick(1, slice(0, S))
+        scatter(win1[3], list1, 3, slice(0, S))
+        finish_plane1(2, new_plane("res", "a"))
+
+        res_bf.append(shared([P, T], BF16, "res_bf", "win2"))
+        for tile, half in zip(xr_last, cuts(T, 1024)):
+            nc.vector.tensor_tensor(res_bf[LAST][:, half], tile[:], win1[LAST][:, half], ADD)
+        w2 = shared([P, K], I32, "w2", "d")
+        w2s = shared([P, K], U8, "w2s", "e")
+        nc.vector.tensor_copy(
+            w2[:].rearrange("p (t m) -> p m t", t=PLANES), w2_raw[:].rearrange("p (m t) -> p m t", t=PLANES)
+        )
+        by_plane(w2s[:], w2s_raw[:])
+
+        sums = sums[:2] + [shared([P, S], F32, "sums", tag) for tag in ("win0", "win1")]
+
+        def product2(t, slots):
+            bank = new_bank(slots.stop - slots.start)
+            product(bank[:], w2[:, span(t, P)].bitcast(FP8X4), w2s[:, span(t, P)], rw[:, slots], rs[:, slots])
+            return bank
+
+        def gate2_piece(t, slots):
+            nc.scalar.copy(sums[t][:, slots], product2(t, slots)[:])
+            gate_on_gpsimd(t, g2, slots)
+
+        for piece, slots in enumerate(PIECES1):
+            pick(LAST - 1, slots)
+            pick(LAST, slots)
             nc.vector.quantize_mx(
                 rw[:, slots].bitcast(FP8X4), rs[:, slots], picked[:, slots, :].rearrange("p s t -> p (s t)")
             )
-            nc.vector.tensor_tensor(gated[0][:, slots], product2(0, slots)[:], g2[:, slots], MULT)
-            nc.vector.tensor_copy(win2[0][:].indirect(offsets(list2, slots)), gated[0][:, slots])
-        for c in range(T // CHUNK):
-            cols = span(c, CHUNK)
-            nc.vector.tensor_tensor(res[last][:, cols], res[last][:, cols], win1[last][:, cols], ADD)
-        win2.append(windows.tile([P, T], F32, name="win", tag="win"))
-
-        def gate_whole(t):
-            for h in range(S // BANK):
-                slots = span(h, BANK)
-                nc.scalar.copy(sums[t][:, slots], product2(t, slots)[:])
-            nc.gpsimd.tensor_tensor(gated[t][:], sums[t][:], g2[:], MULT)
-
-        gate_whole(1)
+            if piece == 0:
+                nc.vector.tensor_tensor(gated[0][:, slots], product2(0, slots)[:], g2[:, slots], MULT)
+            else:
+                gate2_piece(0, slots)
+        for slots in PIECES1:
+            scatter(win2[0], list2, 0, slots)
+        for cols in cuts(T, 512):
+            nc.vector.tensor_tensor(res[LAST][:, cols], res[LAST][:, cols], win1[LAST][:, cols], ADD)
+        for slots in HALVES:
+            gate2_piece(1, slots)
+        win2.append(new_plane("win2", "win2"))
         scalar_zero(win2[1])
-        for t in range(1, PLANES):
-            if t + 1 < PLANES:
-                gate_whole(t + 1)
-                scalar_zero(win2[t + 1])
-            nc.vector.tensor_copy(win2[t][:].indirect(list2[:]), gated[t][:])
-            done = t - 1
-            for c in range(T // CHUNK):
-                cols = span(c, CHUNK)
-                nc.gpsimd.tensor_tensor(res[done][:, cols], res[done][:, cols], win2[done][:, cols], ADD)
-            nc.sync.dma_start(out_planes[:, done, :], res[done][:])
-        for c in range(T // CHUNK):
-            cols = span(c, CHUNK)
-            nc.vector.tensor_tensor(res[last][:, cols], res[last][:, cols], win2[last][:, cols], ADD)
-            nc.sync.dma_start(out_planes[:, last, cols], res[last][:, cols])
+        for slots in HALVES:
+            scatter(win2[1], list2, 1, slots)
+
+        def gate_plane2(t):
+            for slots in HALVES:
+                nc.scalar.copy(sums[t][:, slots], product2(t, slots)[:])
+            gate_on_gpsimd(t, g2, slice(0, S))
+
+        def finish_plane2(t, total):
+            for half in cuts(T, 1024):
+                nc.gpsimd.tensor_tensor(total[:, half], res[t][:, half], win2[t][:, half], ADD)
+                nc.sync.dma_start(out_planes[:, t, half], total[:, half])
+
+        gate_plane2(2)
+        win2.append(new_plane("win2", "picked"))
+        scalar_zero(win2[2])
+        finish_plane2(0, new_plane("total", "win0"))
+        gate_plane2(3)
+        win2.append(new_plane("win2", "win4"))
+        scalar_zero(win2[3])
+        scatter(win2[2], list2, 2, slice(0, S))
+        finish_plane2(1, new_plane("total", "win1"))
+        scatter(win2[3], list2, 3, slice(0, S))
+        finish_plane2(2, new_plane("total", "sums3"))
+        for cols in TAIL:
+            nc.vector.tensor_tensor(res[LAST][:, cols], res[LAST][:, cols], win2[LAST][:, cols], ADD)
+            nc.sync.dma_start(out_planes[:, LAST, cols], res[LAST][:, cols])

@@ -1,6 +1,7 @@
 from contextlib import ExitStack
 
 import concourse.mybir as mybir
+from concourse.masks import make_identity
 
 K, T, S = 512, 2048, 1024
 FLOPS = 2 * 2 * K * K * S
@@ -47,7 +48,8 @@ def tile_moe_mod_none_kernel(
 
     with ExitStack() as ctx:
         keep = ctx.enter_context(tc.tile_pool(name="keep", bufs=1))
-        psum = ctx.enter_context(tc.psum_pool(name="psum", bufs=8))
+        psum = ctx.enter_context(tc.psum_pool(name="psum", bufs=5))
+        turns = ctx.enter_context(tc.psum_pool(name="turns", bufs=3))
 
         def shared(shape, dtype, name, tag):
             return keep.tile(shape, dtype, name=name, tag=tag, align_bytes=64)
@@ -62,11 +64,15 @@ def tile_moe_mod_none_kernel(
         w1 = shared([P, 2 * K], U8, "w1", "f")
         w1s = shared([P, K], U8, "w1s", "g")
         g1 = keep.tile([P, S], F32, name="g1")
-        zero = keep.tile([P, 8], F32, name="zero")
-        res_bf = [keep.tile([P, T], BF16, name="res_bf%d" % t) for t in range(LAST)]
+        zero = keep.tile([P, 512], F32, name="zero")
+        res_bf = [keep.tile([P, T], BF16, name="res_bf%d" % t) for t in range(2)]
+        ident = keep.tile([P, P], F32, name="ident")
         sums = [shared([P, S], F32, "sums", "sums%d" % t) for t in range(PLANES)]
         gated = [keep.tile([P, S], F32, name="gated%d" % t) for t in range(PLANES)]
-        picked = shared([P, S, PLANES], BF16, "picked", "picked")
+        picked = [
+            shared([P, slots.stop - slots.start, PLANES], BF16, "picked", "picked%d" % piece)
+            for piece, slots in enumerate(PIECES1)
+        ]
         rw = keep.tile([P, S], U32, name="rw", align_bytes=64)
         rs = keep.tile([P, S], U8, name="rs", align_bytes=64)
 
@@ -87,7 +93,12 @@ def tile_moe_mod_none_kernel(
 
         def scalar_zero(window):
             for cols in cuts(T, 512):
-                nc.scalar.activation(window[:, cols], zero[:, 0:1].to_broadcast([P, 512]), COPY)
+                nc.scalar.activation(window[:, cols], zero[:], COPY)
+
+        def dma_zero(window):
+            nc.sync.dma_start(
+                window[:].rearrange("p (c n) -> p c n", n=512), zero[:].unsqueeze(1).broadcast_to([P, T // 512, 512])
+            )
 
         def product(bank, w_words, w_scales, words, scales):
             nc.tensor.matmul_mx(
@@ -115,14 +126,12 @@ def tile_moe_mod_none_kernel(
         nc.sync.dma_start(g1[:], gate1)
         nc.sync.dma_start(list2[:], offs2)
 
-        win1 = [new_plane("win1", "win%d" % t) for t in range(PLANES)]
-        win2 = [new_plane("win2", "win4")]
+        win1 = [new_plane("win1", "win%d" % t) for t in range(LAST)]
         scalar_zero(win1[0])
         scalar_zero(win1[1])
-        nc.vector.memset(win1[3][:], 0.0)
         nc.vector.memset(win1[2][:], 0.0)
-        for half in cuts(T, 1024):
-            nc.gpsimd.tensor_scalar(win2[0][:, half], win1[2][:, half], 1.0, 0.0, MULT, ADD)
+
+        make_identity(nc, ident[:])
 
         by_plane(w1[:].bitcast(U16), w1_raw[:].bitcast(U16))
         nc.vector.tensor_copy(xs_slots[:], xs[:].indirect(list1[:]))
@@ -176,33 +185,51 @@ def tile_moe_mod_none_kernel(
                 nc.scalar.copy(res_bf[t][:, cols], total[:, cols])
             res[t] = total
 
-        def pick(t, slots):
-            nc.scalar.activation(picked[:, slots, t], res_bf[t][:].indirect(offsets(list2, slots)), COPY)
+        def pick(t, piece):
+            nc.scalar.activation(picked[piece][:, :, t], res_bf[t][:].indirect(offsets(list2, PIECES1[piece])), COPY)
+
+        win2 = []
+
+        def zero_window2(tag):
+            win2.append(new_plane("win2", tag))
+            dma_zero(win2[-1])
 
         gate_plane1(1)
         gate_plane1(2)
         scatter(win1[1], list1, 1, slice(0, S))
         finish_plane1(0, new_plane("res", "sums2"))
         gate_plane1(3)
-        load_plane("c")
-        w2_raw = shared([P, K], I32, "w2_raw", "f")
-        w2s_raw = shared([P, K], U8, "w2s_raw", "g")
-        g2 = shared([P, S], F32, "g2", "h")
+        win1.append(new_plane("win1", "c"))
+        dma_zero(win1[LAST])
+        xr_third = shared([P, T], F32, "xr_third", "sums0")
+        nc.sync.dma_start(xr_third[:], xr_planes[:, 2, :])
         xr_last = [shared([P, 1024], F32, "xr_last", tag) for tag in "de"]
         for tile, half in zip(xr_last, cuts(T, 1024)):
             nc.sync.dma_start(tile[:], xr_planes[:, LAST, half])
+        w2_raw = shared([P, K], I32, "w2_raw", "f")
+        w2s_raw = shared([P, K], U8, "w2s_raw", "g")
+        g2 = shared([P, S], F32, "g2", "h")
         nc.sync.dma_start(w2_raw[:], w2_words[0].rearrange("p n d -> p (n d)").bitcast(I32))
         load_scales(w2s_raw, w2_scales)
         nc.sync.dma_start(g2[:], gate2)
+        zero_window2("win0")
+        load_plane("sums1")
         load_plane("b")
-        pick(0, slice(0, S))
+        for piece in range(3):
+            pick(0, piece)
         scatter(win1[2], list1, 2, slice(0, S))
         finish_plane1(1, new_plane("res", "sums3"))
-        pick(1, slice(0, S))
+        zero_window2("win1")
+        for piece in range(3):
+            pick(1, piece)
         scatter(win1[3], list1, 3, slice(0, S))
-        finish_plane1(2, new_plane("res", "a"))
+        res_bf.append(shared([P, T], BF16, "res_bf", "a"))
+        for half in cuts(T, 1024):
+            nc.gpsimd.tensor_tensor(res_bf[2][:, half], xr_third[:, half], win1[2][:, half], ADD)
+        for piece in range(3):
+            pick(2, piece)
 
-        res_bf.append(shared([P, T], BF16, "res_bf", "win2"))
+        res_bf.append(shared([P, T], BF16, "res_bf", "sums0"))
         for tile, half in zip(xr_last, cuts(T, 1024)):
             nc.vector.tensor_tensor(res_bf[LAST][:, half], tile[:], win1[LAST][:, half], ADD)
         w2 = shared([P, K], I32, "w2", "d")
@@ -211,38 +238,29 @@ def tile_moe_mod_none_kernel(
             w2[:].rearrange("p (t m) -> p m t", t=PLANES), w2_raw[:].rearrange("p (m t) -> p m t", t=PLANES)
         )
         by_plane(w2s[:], w2s_raw[:])
+        zero_window2("g")
+        zero_window2("f")
 
-        sums = sums[:2] + [shared([P, S], F32, "sums", tag) for tag in ("win0", "win1")]
+        sums = [shared([P, S], F32, "sums", "late%d" % t) for t in range(PLANES)]
 
         def product2(t, slots):
             bank = new_bank(slots.stop - slots.start)
             product(bank[:], w2[:, span(t, P)].bitcast(FP8X4), w2s[:, span(t, P)], rw[:, slots], rs[:, slots])
             return bank
 
-        def gate2_piece(t, slots):
-            nc.scalar.copy(sums[t][:, slots], product2(t, slots)[:])
-            gate_on_gpsimd(t, g2, slots)
-
         for piece, slots in enumerate(PIECES1):
-            pick(LAST - 1, slots)
-            pick(LAST, slots)
+            pick(LAST, piece)
             nc.vector.quantize_mx(
-                rw[:, slots].bitcast(FP8X4), rs[:, slots], picked[:, slots, :].rearrange("p s t -> p (s t)")
+                rw[:, slots].bitcast(FP8X4), rs[:, slots], picked[piece][:].rearrange("p s t -> p (s t)")
             )
-            if piece == 0:
-                nc.vector.tensor_tensor(gated[0][:, slots], product2(0, slots)[:], g2[:, slots], MULT)
-            else:
-                gate2_piece(0, slots)
-        for slots in PIECES1:
+        for q, slots in enumerate(QUARTERS[:2]):
+            early = shared([P, 256], F32, "early", "picked%d" % (q + 1))
+            nc.vector.tensor_tensor(early[:], product2(0, slots)[:], g2[:, slots], MULT)
+            nc.vector.tensor_copy(win2[0][:].indirect(offsets(list2, slots)), early[:])
+        for slots in QUARTERS[2:]:
+            nc.scalar.copy(sums[0][:, slots], product2(0, slots)[:])
+            gate_on_gpsimd(0, g2, slots)
             scatter(win2[0], list2, 0, slots)
-        for cols in cuts(T, 512):
-            nc.vector.tensor_tensor(res[LAST][:, cols], res[LAST][:, cols], win1[LAST][:, cols], ADD)
-        for slots in HALVES:
-            gate2_piece(1, slots)
-        win2.append(new_plane("win2", "win2"))
-        scalar_zero(win2[1])
-        for slots in HALVES:
-            scatter(win2[1], list2, 1, slots)
 
         def gate_plane2(t):
             for slots in HALVES:
@@ -254,15 +272,33 @@ def tile_moe_mod_none_kernel(
                 nc.gpsimd.tensor_tensor(total[:, half], res[t][:, half], win2[t][:, half], ADD)
                 nc.sync.dma_start(out_planes[:, t, half], total[:, half])
 
+        def sum_by_transposes(t):
+            turned = new_plane("turned", "late1")
+            total = new_plane("res", "res%d" % t)
+            for cols in cuts(T, BANK):
+                blocks = [slice(cols.start + b.start, cols.start + b.stop) for b in cuts(BANK, P)]
+                bank = turns.tile([P, BANK], F32, name="turn", tag="turn")
+                for at, block in zip(cuts(BANK, P), blocks):
+                    for term, first in ((res[t], True), (win1[t], False)):
+                        nc.tensor.matmul(
+                            bank[:, at], lhsT=term[:, block], rhs=ident[:], is_transpose=True, start=first, stop=not first
+                        )
+                nc.scalar.copy(turned[:, cols], bank[:])
+                bank = turns.tile([P, BANK], F32, name="turn", tag="turn")
+                for at, block in zip(cuts(BANK, P), blocks):
+                    nc.tensor.transpose(bank[:, at], turned[:, block], ident[:])
+                nc.scalar.copy(total[:, cols], bank[:])
+            res[t] = total
+
+        gate_plane2(1)
         gate_plane2(2)
-        win2.append(new_plane("win2", "picked"))
-        scalar_zero(win2[2])
-        finish_plane2(0, new_plane("total", "win0"))
+        sum_by_transposes(2)
+        sum_by_transposes(3)
+        scatter(win2[1], list2, 1, slice(0, S))
+        finish_plane2(0, new_plane("total", "late2"))
         gate_plane2(3)
-        win2.append(new_plane("win2", "win4"))
-        scalar_zero(win2[3])
         scatter(win2[2], list2, 2, slice(0, S))
-        finish_plane2(1, new_plane("total", "win1"))
+        finish_plane2(1, new_plane("total", "late3"))
         scatter(win2[3], list2, 3, slice(0, S))
         finish_plane2(2, new_plane("total", "sums3"))
         for cols in TAIL:

from contextlib import ExitStack

import concourse.mybir as mybir
from concourse.masks import make_identity

K, T, S = 512, 2048, 1024
FLOPS = 2 * 2 * K * K * S

F32 = mybir.dt.float32
BF16 = mybir.dt.bfloat16
I32 = mybir.dt.int32
U32 = mybir.dt.uint32
U16 = mybir.dt.uint16
U8 = mybir.dt.uint8
FP8X4 = mybir.dt.float8_e4m3fn_x4
FP4X4 = mybir.dt.float4_e2m1fn_x4
MULT = mybir.AluOpType.mult
ADD = mybir.AluOpType.add
COPY = mybir.ActivationFunctionType.Copy

P = 128
PLANES = 4
LAST = PLANES - 1
PER_COL = 16
BANK = 512


def span(i, width):
    return slice(i * width, (i + 1) * width)


def cuts(total, width):
    return [span(i, width) for i in range(total // width)]


PIECES1 = [slice(0, 256), slice(256, 512), slice(512, 1024)]
QUARTERS = cuts(S, 256)
HALVES = cuts(S, BANK)
TAIL = [slice(0, 640), slice(640, 1280), slice(1280, 1792), slice(1792, 2048)]


def tile_moe_mod_none_kernel(
    tc, x_words, x_scales, xr, w1_words, w1_scales, w2_words, w2_scales, gate1, gate2, offs, offs2, out
):
    nc = tc.nc
    xr_planes = xr.rearrange("(p t) n -> p t n", t=PLANES)
    out_planes = out.rearrange("(p t) n -> p t n", t=PLANES)

    with ExitStack() as ctx:
        keep = ctx.enter_context(tc.tile_pool(name="keep", bufs=1))
        psum = ctx.enter_context(tc.psum_pool(name="psum", bufs=5))
        turns = ctx.enter_context(tc.psum_pool(name="turns", bufs=3))

        def shared(shape, dtype, name, tag):
            return keep.tile(shape, dtype, name=name, tag=tag, align_bytes=64)

        list1 = keep.tile([P, S // PER_COL], U16, name="list1")
        list2 = keep.tile([P, S // PER_COL], U16, name="list2")
        xw = shared([P, T], I32, "xw", "a")
        xs = shared([P, T], U8, "xs", "b")
        xs_slots = shared([P, S], U8, "xs_slots", "c")
        w1_raw = shared([P, 2 * K], U8, "w1_raw", "d")
        w1s_raw = shared([P, K], U8, "w1s_raw", "e")
        w1 = shared([P, 2 * K], U8, "w1", "f")
        w1s = shared([P, K], U8, "w1s", "g")
        g1 = keep.tile([P, S], F32, name="g1")
        zero = keep.tile([P, 512], F32, name="zero")
        res_bf = [keep.tile([P, T], BF16, name="res_bf%d" % t) for t in range(2)]
        ident = keep.tile([P, P], F32, name="ident")
        sums = [shared([P, S], F32, "sums", "sums%d" % t) for t in range(PLANES)]
        gated = [keep.tile([P, S], F32, name="gated%d" % t) for t in range(PLANES)]
        picked = [
            shared([P, slots.stop - slots.start, PLANES], BF16, "picked", "picked%d" % piece)
            for piece, slots in enumerate(PIECES1)
        ]
        rw = keep.tile([P, S], U32, name="rw", align_bytes=64)
        rs = keep.tile([P, S], U8, name="rs", align_bytes=64)

        def load_scales(plane, rows):
            for q in range(4):
                four = rows[0, span(q, 4), :].bitcast(I32)
                nc.sync.dma_start(
                    plane[span(q, 32), :].bitcast(I32), four.unsqueeze(0).broadcast_to([8, 4, four.shape[1]])
                )

        def offsets(lst, slots):
            return lst[:, slots.start // PER_COL : slots.stop // PER_COL]

        def by_plane(dst, src):
            nc.vector.tensor_copy(
                dst.rearrange("p (t m) -> p t m", t=PLANES), src.rearrange("p (m t) -> p t m", t=PLANES)
            )

        def scalar_zero(window):
            for cols in cuts(T, 512):
                nc.scalar.activation(window[:, cols], zero[:], COPY)

        def dma_zero(window):
            nc.sync.dma_start(
                window[:].rearrange("p (c n) -> p c n", n=512), zero[:].unsqueeze(1).broadcast_to([P, T // 512, 512])
            )

        def product(bank, w_words, w_scales, words, scales):
            nc.tensor.matmul_mx(
                bank, lhsT=w_words, lhsT_scale=w_scales, rhs=words.bitcast(FP8X4), rhs_scale=scales, start=True, stop=True
            )

        def new_bank(width):
            return psum.tile([P, width], F32, name="bank", tag="bank")

        def new_plane(name, tag):
            return shared([P, T], F32, name, tag)

        def gate_on_gpsimd(t, gate, slots):
            nc.gpsimd.tensor_tensor(gated[t][:, slots], sums[t][:, slots], gate[:, slots], MULT)

        def scatter(window, lst, t, slots):
            nc.vector.tensor_copy(window[:].indirect(offsets(lst, slots)), gated[t][:, slots])

        nc.vector.memset(zero[:], 0.0)
        nc.sync.dma_start(w1_raw[:].bitcast(I32), w1_words[0].bitcast(I32))
        load_scales(xs, x_scales)
        nc.sync.dma_start(list1[:], offs)
        nc.sync.dma_start(xw[:], x_words[0].rearrange("p t d -> p (t d)").bitcast(I32))
        load_scales(w1s_raw, w1_scales)
        nc.sync.dma_start(g1[:], gate1)
        nc.sync.dma_start(list2[:], offs2)

        win1 = [new_plane("win1", "win%d" % t) for t in range(LAST)]
        scalar_zero(win1[0])
        scalar_zero(win1[1])
        nc.vector.memset(win1[2][:], 0.0)

        make_identity(nc, ident[:])

        by_plane(w1[:].bitcast(U16), w1_raw[:].bitcast(U16))
        nc.vector.tensor_copy(xs_slots[:], xs[:].indirect(list1[:]))
        by_plane(w1s[:], w1s_raw[:])
        xw_slots = []
        for slots, tag in zip(PIECES1, "hde"):
            xw_slots.append(shared([P, slots.stop - slots.start], U32, "xw_slots", tag))
            nc.vector.tensor_copy(xw_slots[-1][:], xw[:].bitcast(U32).indirect(offsets(list1, slots)))

        res = []

        def load_plane(tag):
            res.append(shared([P, T], F32, "res", tag))
            nc.sync.dma_start(res[-1][:], xr_planes[:, len(res) - 1, :])

        load_plane("b")
        load_plane("a")

        def product1(bank, t, piece):
            product(
                bank,
                w1[:, span(t, 2 * P)].bitcast(FP4X4),
                w1s[:, span(t, P)],
                xw_slots[piece][:],
                xs_slots[:, PIECES1[piece]],
            )

        for piece, slots in enumerate(PIECES1):
            bank = new_bank(slots.stop - slots.start)
            product1(bank[:], 0, piece)
            if piece == 0:
                nc.vector.tensor_tensor(gated[0][:, slots], bank[:], g1[:, slots], MULT)
            else:
                nc.scalar.copy(sums[0][:, slots], bank[:])
                gate_on_gpsimd(0, g1, slots)
            scatter(win1[0], list1, 0, slots)

        def gate_plane1(t):
            low, high = new_bank(BANK), new_bank(BANK)
            product1(low[:, PIECES1[0]], t, 0)
            product1(low[:, PIECES1[1]], t, 1)
            product1(high[:], t, 2)
            nc.scalar.copy(sums[t][:, HALVES[0]], low[:])
            nc.scalar.copy(sums[t][:, HALVES[1]], high[:])
            gate_on_gpsimd(t, g1, slice(0, S))

        def finish_plane1(t, total):
            for half in cuts(T, 1024):
                nc.gpsimd.tensor_tensor(total[:, half], res[t][:, half], win1[t][:, half], ADD)
            for cols in cuts(T, 512):
                nc.scalar.copy(res_bf[t][:, cols], total[:, cols])
            res[t] = total

        def pick(t, piece):
            nc.scalar.activation(picked[piece][:, :, t], res_bf[t][:].indirect(offsets(list2, PIECES1[piece])), COPY)

        win2 = []

        def zero_window2(tag):
            win2.append(new_plane("win2", tag))
            dma_zero(win2[-1])

        gate_plane1(1)
        gate_plane1(2)
        scatter(win1[1], list1, 1, slice(0, S))
        finish_plane1(0, new_plane("res", "sums2"))
        gate_plane1(3)
        win1.append(new_plane("win1", "c"))
        dma_zero(win1[LAST])
        xr_third = shared([P, T], F32, "xr_third", "sums0")
        nc.sync.dma_start(xr_third[:], xr_planes[:, 2, :])
        xr_last = [shared([P, 1024], F32, "xr_last", tag) for tag in "de"]
        for tile, half in zip(xr_last, cuts(T, 1024)):
            nc.sync.dma_start(tile[:], xr_planes[:, LAST, half])
        w2_raw = shared([P, K], I32, "w2_raw", "f")
        w2s_raw = shared([P, K], U8, "w2s_raw", "g")
        g2 = shared([P, S], F32, "g2", "h")
        nc.sync.dma_start(w2_raw[:], w2_words[0].rearrange("p n d -> p (n d)").bitcast(I32))
        load_scales(w2s_raw, w2_scales)
        nc.sync.dma_start(g2[:], gate2)
        zero_window2("win0")
        load_plane("sums1")
        load_plane("b")
        for piece in range(3):
            pick(0, piece)
        scatter(win1[2], list1, 2, slice(0, S))
        finish_plane1(1, new_plane("res", "sums3"))
        zero_window2("win1")
        for piece in range(3):
            pick(1, piece)
        scatter(win1[3], list1, 3, slice(0, S))
        res_bf.append(shared([P, T], BF16, "res_bf", "a"))
        for half in cuts(T, 1024):
            nc.gpsimd.tensor_tensor(res_bf[2][:, half], xr_third[:, half], win1[2][:, half], ADD)
        for piece in range(3):
            pick(2, piece)

        res_bf.append(shared([P, T], BF16, "res_bf", "sums0"))
        for tile, half in zip(xr_last, cuts(T, 1024)):
            nc.vector.tensor_tensor(res_bf[LAST][:, half], tile[:], win1[LAST][:, half], ADD)
        w2 = shared([P, K], I32, "w2", "d")
        w2s = shared([P, K], U8, "w2s", "e")
        nc.vector.tensor_copy(
            w2[:].rearrange("p (t m) -> p m t", t=PLANES), w2_raw[:].rearrange("p (m t) -> p m t", t=PLANES)
        )
        by_plane(w2s[:], w2s_raw[:])
        zero_window2("g")
        zero_window2("f")

        sums = [shared([P, S], F32, "sums", "late%d" % t) for t in range(PLANES)]

        def product2(t, slots):
            bank = new_bank(slots.stop - slots.start)
            product(bank[:], w2[:, span(t, P)].bitcast(FP8X4), w2s[:, span(t, P)], rw[:, slots], rs[:, slots])
            return bank

        for piece, slots in enumerate(PIECES1):
            pick(LAST, piece)
            nc.vector.quantize_mx(
                rw[:, slots].bitcast(FP8X4), rs[:, slots], picked[piece][:].rearrange("p s t -> p (s t)")
            )
        for q, slots in enumerate(QUARTERS[:2]):
            early = shared([P, 256], F32, "early", "picked%d" % (q + 1))
            nc.vector.tensor_tensor(early[:], product2(0, slots)[:], g2[:, slots], MULT)
            nc.vector.tensor_copy(win2[0][:].indirect(offsets(list2, slots)), early[:])
        for slots in QUARTERS[2:]:
            nc.scalar.copy(sums[0][:, slots], product2(0, slots)[:])
            gate_on_gpsimd(0, g2, slots)
            scatter(win2[0], list2, 0, slots)

        def gate_plane2(t):
            for slots in HALVES:
                nc.scalar.copy(sums[t][:, slots], product2(t, slots)[:])
            gate_on_gpsimd(t, g2, slice(0, S))

        def finish_plane2(t, total):
            for half in cuts(T, 1024):
                nc.gpsimd.tensor_tensor(total[:, half], res[t][:, half], win2[t][:, half], ADD)
                nc.sync.dma_start(out_planes[:, t, half], total[:, half])

        def sum_by_transposes(t):
            turned = new_plane("turned", "late1")
            total = new_plane("res", "res%d" % t)
            for cols in cuts(T, BANK):
                blocks = [slice(cols.start + b.start, cols.start + b.stop) for b in cuts(BANK, P)]
                bank = turns.tile([P, BANK], F32, name="turn", tag="turn")
                for at, block in zip(cuts(BANK, P), blocks):
                    for term, first in ((res[t], True), (win1[t], False)):
                        nc.tensor.matmul(
                            bank[:, at], lhsT=term[:, block], rhs=ident[:], is_transpose=True, start=first, stop=not first
                        )
                nc.scalar.copy(turned[:, cols], bank[:])
                bank = turns.tile([P, BANK], F32, name="turn", tag="turn")
                for at, block in zip(cuts(BANK, P), blocks):
                    nc.tensor.transpose(bank[:, at], turned[:, block], ident[:])
                nc.scalar.copy(total[:, cols], bank[:])
            res[t] = total

        gate_plane2(1)
        gate_plane2(2)
        sum_by_transposes(2)
        sum_by_transposes(3)
        scatter(win2[1], list2, 1, slice(0, S))
        finish_plane2(0, new_plane("total", "late2"))
        gate_plane2(3)
        scatter(win2[2], list2, 2, slice(0, S))
        finish_plane2(1, new_plane("total", "late3"))
        scatter(win2[3], list2, 3, slice(0, S))
        finish_plane2(2, new_plane("total", "sums3"))
        for cols in TAIL:
            nc.vector.tensor_tensor(res[LAST][:, cols], res[LAST][:, cols], win2[LAST][:, cols], ADD)
            nc.sync.dma_start(out_planes[:, LAST, cols], res[LAST][:, cols])
